import numpy as np
import ml_dtypes


def mxq(x, axis, fmt="e4m3"):
    dtype, down = {"e4m3": (ml_dtypes.float8_e4m3fn, 7), "e5m2": (ml_dtypes.float8_e5m2, 14)}[fmt]
    v = np.moveaxis(np.asarray(x, np.float32).astype(ml_dtypes.bfloat16).astype(np.float64), axis, -1)
    blocks = v.reshape(v.shape[:-1] + (-1, 32))
    amax = np.abs(blocks).max(-1, keepdims=True)
    byte = np.maximum(np.where(amax > 0, np.frexp(amax)[1] - 1 + 127, 0) - down, 1)
    scale = np.exp2(byte - 127.0)
    codes = (blocks / scale).astype(np.float32).astype(dtype).astype(np.float64)
    return np.moveaxis((codes * scale).reshape(v.shape), -1, axis)


WIDE = False


def mx_kscale(k, group=512):
    if not WIDE:
        return np.ones(k)
    levels = np.array([18, -18])
    if group != 512:
        return np.exp2(np.random.permutation(np.resize(levels, k // group))).repeat(group)
    if k % 512:
        return np.exp2(np.random.permutation(np.resize(levels, k // 32))).repeat(32)
    a = np.empty((k // 512, 16))
    for p in range(k // 512):
        a[p, :8] = np.random.permutation(np.resize(levels, 8))
        for g in range(8):
            far = levels[np.abs(levels - a[p, g]) >= 10]
            a[p, g + 8] = far[np.random.randint(len(far))]
    return np.exp2(a.ravel()).repeat(32)


def f64(x):
    return np.asarray(x).astype(np.float64)


G, D, M, N = 4, 128, 128, 512


def setup_inputs():
    n = np.random.standard_normal
    s_d = mx_kscale(D, 0)
    return {
        "x": (n((G, D, N)) * s_d[:, None]).astype(np.float32),
        "w1": (n((G, D, M)) / np.sqrt(D) / s_d[:, None]).astype(np.float32),
        "w2": (n((G, D, M)) / np.sqrt(D) / s_d[:, None]).astype(np.float32),
        "fl": (np.random.uniform(0.05, 0.3, (G, M, 1))).astype(np.float32),
        "dx": (n((G, D, N)) * s_d[:, None]).astype(np.float32),
        "og": (np.random.uniform(0.5, 2.0, (G, M, 1))).astype(np.float32),
        "base": (0.3 * n((G, M, N))).astype(np.float32),
    }


def reference(x, w1, w2, fl, dx, og, base):
    w1q = mxq(f64(w1), 1, "e4m3")
    xq = mxq(f64(x), 1, "e4m3")
    z1 = w1q.transpose(0, 2, 1) @ xq
    dxq = mxq(f64(dx), 1, "e4m3")
    tz1 = w1q.transpose(0, 2, 1) @ dxq
    w2q = mxq(f64(w2), 1, "e4m3")
    z2 = w2q.transpose(0, 2, 1) @ xq
    tz2 = w2q.transpose(0, 2, 1) @ dxq
    e1 = np.exp(np.square(z1) * (-1.0))
    e2 = np.exp(np.square(z2) * (-1.0))
    xe1 = tz1 * z1 * 2.0 * (-1.0) * e1
    xe2 = tz2 * z2 * 2.0 * (-1.0) * e2
    xh = (xe1 - (xe1 + xe2) * e1 / (e1 + e2 + f64(fl))) / (e1 + e2 + f64(fl)) * z2 + tz2 * e1 / (e1 + e2 + f64(fl))
    y = xh * f64(og) + f64(base)
    return y

@@ -1,0 +1,209 @@
+from contextlib import ExitStack
+
+import concourse.mybir as mybir
+
+G, D, M, N = 4, 128, 128, 512
+FLOPS = 4 * 2 * G * D * M * N
+
+F32 = mybir.dt.float32
+BF16 = mybir.dt.bfloat16
+U32 = mybir.dt.uint32
+U8 = mybir.dt.uint8
+FP8X4 = mybir.dt.float8_e4m3fn_x4
+ALU = mybir.AluOpType
+ACT = mybir.ActivationFunctionType
+
+P = 128
+PACK = 4
+ROWS = D // PACK
+RUN = 4
+X_SPLIT = 344
+SMALLEST_FLOOR = 2.0**-60
+
+
+def tile_rows_tngaussshare_kernel(tc, x, w1, w2, fl, dx, og, base, out):
+    nc = tc.nc
+    with ExitStack() as ctx:
+        sb = ctx.enter_context(tc.tile_pool(name="sb", bufs=1))
+        ps = ctx.enter_context(tc.psum_pool(name="ps", bufs=1))
+        ctx.enter_context(tc.manual_schedule())
+
+        def load_rows(name, src, width):
+            raw = sb.tile([P, PACK, width], F32, name=name + "_raw")
+            nc.sync.dma_start(out=raw[:], in_=src.rearrange("g (p j) n -> (g p) j n", j=PACK))
+            return raw
+
+        def interleave(copy, grouped, raw, lo, hi):
+            copy(
+                out=grouped[:, lo:hi, :].rearrange("p (c i) j -> p c j i", i=RUN),
+                in_=raw[:, :, lo:hi].rearrange("p j (c i) -> p c j i", i=RUN),
+            )
+
+        def quantize(name, grouped, width):
+            codes = sb.tile([P, width], U32, name=name + "_codes", align_bytes=64)
+            scales = sb.tile([P, width], U8, name=name + "_scales", align_bytes=64)
+            nc.vector.quantize_mx(
+                out=codes[:].bitcast(FP8X4),
+                scales=scales[:],
+                in_=grouped[:].rearrange("p n j -> p (n j)"),
+            )
+            return codes, scales
+
+        def product(bank, g, weights, moving):
+            rows = slice(ROWS * g, ROWS * (g + 1))
+            nc.tensor.matmul_mx(
+                out=bank[:],
+                lhsT=weights[0][rows, :].bitcast(FP8X4),
+                lhsT_scale=weights[1][rows, :],
+                rhs=moving[0][rows, :].bitcast(FP8X4),
+                rhs_scale=moving[1][rows, :],
+                start=True,
+                stop=True,
+            )
+
+        def per_group(name):
+            return [sb.tile([P, N], F32, name="%s%d" % (name, g)) for g in range(G)]
+
+        small_rows = sb.tile([P, 2 * G * 32], F32, align_bytes=64)
+        small_cols = sb.tile([P, 2 * G * 32], F32, align_bytes=64)
+        nc.vector.memset(small_rows[:], 0.0)
+        w2_raw = load_rows("w2", w2, M)
+        for k, vec in enumerate((fl, og)):
+            nc.sync.dma_start(
+                out=small_rows[0:P:32, k * G * 32 : (k + 1) * G * 32].rearrange("q (g i) -> q g i", i=32),
+                in_=vec.rearrange("g (q i) o -> q g (i o)", i=32),
+            )
+        x_raw = load_rows("x", x, N)
+        w1_raw = load_rows("w1", w1, M)
+        dx_raw = load_rows("dx", dx, N)
+        base_sb = sb.tile([P, G, N], F32)
+        nc.sync.dma_start(out=base_sb[:], in_=base.rearrange("g m n -> m g n"))
+
+        nc.vector.transpose(small_cols[:], small_rows[:])
+        floor = sb.tile([P, G], F32)
+        nc.vector.tensor_scalar_max(out=floor[:], in0=small_cols[:, 0 : G * 32 : 32], scalar1=SMALLEST_FLOOR)
+        log_fl = sb.tile([P, G], F32)
+        neg_log_fl = sb.tile([P, G], F32)
+        nc.scalar.activation(out=log_fl[:], in_=floor[:], func=ACT.Ln)
+        nc.scalar.mul(out=neg_log_fl[:], in_=log_fl[:], mul=-1.0)
+
+        def gain(g):
+            col = (G + g) * 32
+            return small_cols[:, col : col + 1]
+
+        w2_bf = sb.tile([P, M, PACK], BF16, align_bytes=64)
+        w1_bf = sb.tile([P, M, PACK], BF16, align_bytes=64)
+        x_bf = sb.tile([P, N, PACK], BF16, align_bytes=64)
+        dx_bf = sb.tile([P, N, PACK], BF16, align_bytes=64)
+
+        bank_b = [ps.tile([P, N], F32, name="bank_b%d" % g) for g in range(G)]
+        bank_a = [ps.tile([P, N], F32, name="bank_a%d" % g) for g in range(G)]
+
+        interleave(nc.vector.tensor_copy, w2_bf, w2_raw, 0, M)
+        w2_q = quantize("w2", w2_bf, M)
+        interleave(nc.vector.tensor_copy, x_bf, x_raw, 0, X_SPLIT)
+        interleave(nc.scalar.copy, x_bf, x_raw, X_SPLIT, N)
+        x_q = quantize("x", x_bf, N)
+        for g in range(G):
+            product(bank_b[g], g, w2_q, x_q)
+        interleave(nc.vector.tensor_copy, w1_bf, w1_raw, 0, M)
+        w1_q = quantize("w1", w1_bf, M)
+        for g in range(G):
+            product(bank_a[g], g, w1_q, x_q)
+
+        b_sq = per_group("b_sq")
+        rest = per_group("rest")
+        a_sb = per_group("a_sb")
+        a_sq = per_group("a_sq")
+        log_rest = per_group("log_rest")
+        logit = per_group("logit")
+        share = per_group("share")
+        k1 = per_group("k1")
+        k2 = per_group("k2")
+        m1 = per_group("m1")
+        dz = per_group("dz")
+        u = per_group("u")
+        v = per_group("v")
+        w = per_group("w")
+        y = per_group("y")
+        res = per_group("res")
+
+        def s_bell(g):
+            nc.scalar.activation(out=b_sq[g][:], in_=bank_b[g][:], func=ACT.Square)
+            nc.scalar.activation(out=rest[g][:], in_=b_sq[g][:], func=ACT.Sigmoid, bias=log_fl[:, g : g + 1])
+
+        def copy_a(copy, g):
+            copy(out=a_sb[g][:], in_=bank_a[g][:])
+
+        def v_k1(g):
+            nc.vector.scalar_tensor_tensor(
+                out=k1[g][:], in0=rest[g][:], scalar=-1.0, in1=bank_b[g][:], op0=ALU.add, op1=ALU.mult
+            )
+
+        def v_m1(g):
+            nc.vector.tensor_tensor(out=m1[g][:], in0=a_sb[g][:], in1=bank_a[g][:], op=ALU.mult)
+            product(bank_a[g], g, w2_q, dx_q)
+
+        def v_k2(g):
+            nc.vector.tensor_tensor(out=k2[g][:], in0=k1[g][:], in1=bank_a[g][:], op=ALU.mult)
+            nc.gpsimd.tensor_tensor(out=dz[g][:], in0=k2[g][:], in1=m1[g][:], op=ALU.add)
+
+        def v_u(g):
+            nc.vector.scalar_tensor_tensor(
+                out=u[g][:], in0=dz[g][:], scalar=2.0, in1=bank_b[g][:], op0=ALU.mult, op1=ALU.mult
+            )
+
+        copy_a(nc.vector.tensor_copy, 0)
+        interleave(nc.vector.tensor_copy, dx_bf, dx_raw, 0, N)
+        dx_q = quantize("dx", dx_bf, N)
+        s_bell(0)
+        s_bell(1)
+        copy_a(nc.scalar.copy, 1)
+        s_bell(2)
+        copy_a(nc.scalar.copy, 2)
+        s_bell(3)
+        copy_a(nc.scalar.copy, 3)
+        product(bank_a[0], 0, w1_q, dx_q)
+        product(bank_a[1], 1, w1_q, dx_q)
+        v_k1(0)
+        v_m1(0)
+        product(bank_a[2], 2, w1_q, dx_q)
+        v_k1(1)
+        v_m1(1)
+        product(bank_a[3], 3, w1_q, dx_q)
+        v_k2(0)
+        v_k1(2)
+        v_k2(1)
+        v_m1(2)
+        v_k1(3)
+        v_m1(3)
+        v_k2(2)
+        v_u(0)
+        v_k2(3)
+        v_u(1)
+        v_u(2)
+        v_u(3)
+
+        for g in range(G):
+            nc.scalar.activation(out=a_sq[g][:], in_=a_sb[g][:], func=ACT.Square)
+            nc.scalar.activation(out=log_rest[g][:], in_=rest[g][:], func=ACT.Ln)
+            nc.gpsimd.tensor_tensor(out=logit[g][:], in0=a_sq[g][:], in1=log_rest[g][:], op=ALU.subtract)
+        for g in range(G):
+            nc.scalar.activation(
+                out=share[g][:], in_=logit[g][:], func=ACT.Sigmoid, scale=-1.0, bias=neg_log_fl[:, g : g + 1]
+            )
+
+        for pair in ((0, 1), (2, 3)):
+            for g in pair:
+                nc.vector.scalar_tensor_tensor(
+                    out=v[g][:], in0=share[g][:], scalar=-1.0, in1=u[g][:], op0=ALU.add, op1=ALU.mult
+                )
+            for g in pair:
+                nc.vector.tensor_tensor(out=w[g][:], in0=v[g][:], in1=bank_a[g][:], op=ALU.add)
+            for g in pair:
+                nc.vector.scalar_tensor_tensor(
+                    out=y[g][:], in0=w[g][:], scalar=gain(g), in1=share[g][:], op0=ALU.mult, op1=ALU.mult
+                )
+            for g in pair:
+                nc.vector.tensor_tensor(out=res[g][:], in0=y[g][:], in1=base_sb[:, g, :], op=ALU.add)
+                nc.sync.dma_start(out=out[g], in_=res[g][:])

@@ -79,14 +79,6 @@ def tile_rows_tngaussshare_kernel(tc, x, w1, w2, fl, dx, og, base, out):
         base_sb = sb.tile([P, G, N], F32)
         nc.sync.dma_start(out=base_sb[:], in_=base.rearrange("g m n -> m g n"))
 
-        nc.vector.transpose(small_cols[:], small_rows[:])
-        floor = sb.tile([P, G], F32)
-        nc.vector.tensor_scalar_max(out=floor[:], in0=small_cols[:, 0 : G * 32 : 32], scalar1=SMALLEST_FLOOR)
-        log_fl = sb.tile([P, G], F32)
-        neg_log_fl = sb.tile([P, G], F32)
-        nc.scalar.activation(out=log_fl[:], in_=floor[:], func=ACT.Ln)
-        nc.scalar.mul(out=neg_log_fl[:], in_=log_fl[:], mul=-1.0)
-
         def gain(g):
             col = (G + g) * 32
             return small_cols[:, col : col + 1]
@@ -99,14 +91,23 @@ def tile_rows_tngaussshare_kernel(tc, x, w1, w2, fl, dx, og, base, out):
         bank_b = [ps.tile([P, N], F32, name="bank_b%d" % g) for g in range(G)]
         bank_a = [ps.tile([P, N], F32, name="bank_a%d" % g) for g in range(G)]
 
+        floor = sb.tile([P, G], F32)
+        log_fl = sb.tile([P, G], F32)
+        neg_log_fl = sb.tile([P, G], F32)
+        warm = sb.tile([P, 1], F32)
+        nc.vector.transpose(small_cols[:], small_rows[:])
         interleave(nc.vector.tensor_copy, w2_bf, w2_raw, 0, M)
+        nc.vector.tensor_scalar_max(out=floor[:], in0=small_cols[:, 0 : G * 32 : 32], scalar1=SMALLEST_FLOOR)
         w2_q = quantize("w2", w2_bf, M)
+        nc.scalar.activation(out=log_fl[:], in_=floor[:], func=ACT.Ln)
+        nc.scalar.mul(out=neg_log_fl[:], in_=log_fl[:], mul=-1.0)
         interleave(nc.vector.tensor_copy, x_bf, x_raw, 0, X_SPLIT)
         interleave(nc.scalar.copy, x_bf, x_raw, X_SPLIT, N)
+        nc.scalar.activation(out=warm[:], in_=log_fl[:, 0:1], func=ACT.Sigmoid)
+        interleave(nc.vector.tensor_copy, w1_bf, w1_raw, 0, M)
         x_q = quantize("x", x_bf, N)
         for g in range(G):
             product(bank_b[g], g, w2_q, x_q)
-        interleave(nc.vector.tensor_copy, w1_bf, w1_raw, 0, M)
         w1_q = quantize("w1", w1_bf, M)
         for g in range(G):
             product(bank_a[g], g, w1_q, x_q)
@@ -128,12 +129,20 @@ def tile_rows_tngaussshare_kernel(tc, x, w1, w2, fl, dx, og, base, out):
         y = per_group("y")
         res = per_group("res")
 
-        def s_bell(g):
+        def s_square_b(g):
             nc.scalar.activation(out=b_sq[g][:], in_=bank_b[g][:], func=ACT.Square)
+
+        def s_rest(g):
             nc.scalar.activation(out=rest[g][:], in_=b_sq[g][:], func=ACT.Sigmoid, bias=log_fl[:, g : g + 1])
 
         def copy_a(copy, g):
             copy(out=a_sb[g][:], in_=bank_a[g][:])
+
+        def g_square_a(g):
+            nc.gpsimd.tensor_tensor(out=a_sq[g][:], in0=a_sb[g][:], in1=a_sb[g][:], op=ALU.mult)
+
+        def g_dz(g):
+            nc.gpsimd.tensor_tensor(out=dz[g][:], in0=k2[g][:], in1=m1[g][:], op=ALU.add)
 
         def v_k1(g):
             nc.vector.scalar_tensor_tensor(
@@ -142,56 +151,96 @@ def tile_rows_tngaussshare_kernel(tc, x, w1, w2, fl, dx, og, base, out):
 
         def v_m1(g):
             nc.vector.tensor_tensor(out=m1[g][:], in0=a_sb[g][:], in1=bank_a[g][:], op=ALU.mult)
-            product(bank_a[g], g, w2_q, dx_q)
 
         def v_k2(g):
-            nc.vector.tensor_tensor(out=k2[g][:], in0=k1[g][:], in1=bank_a[g][:], op=ALU.mult)
-            nc.gpsimd.tensor_tensor(out=dz[g][:], in0=k2[g][:], in1=m1[g][:], op=ALU.add)
+            nc.vector.tensor_tensor(out=k2[g][:], in0=k1[g][:], in1=bank_b[g][:], op=ALU.mult)
 
         def v_u(g):
             nc.vector.scalar_tensor_tensor(
                 out=u[g][:], in0=dz[g][:], scalar=2.0, in1=bank_b[g][:], op0=ALU.mult, op1=ALU.mult
             )
 
-        copy_a(nc.vector.tensor_copy, 0)
+        def v_logit(g):
+            nc.vector.tensor_tensor(out=logit[g][:], in0=a_sq[g][:], in1=log_rest[g][:], op=ALU.subtract)
+
+        def ta_to_a(g):
+            product(bank_a[g], g, w1_q, dx_q)
+
+        def tb_to_a(g):
+            product(bank_a[g], g, w2_q, dx_q)
+
+        def tb_to_b(g):
+            product(bank_b[g], g, w2_q, dx_q)
+
+        def b_to_b(g):
+            product(bank_b[g], g, w2_q, x_q)
+
         interleave(nc.vector.tensor_copy, dx_bf, dx_raw, 0, N)
+        copy_a(nc.vector.tensor_copy, 0)
         dx_q = quantize("dx", dx_bf, N)
-        s_bell(0)
-        s_bell(1)
+        s_square_b(0)
+        s_square_b(1)
+        s_rest(0)
+        s_rest(1)
         copy_a(nc.scalar.copy, 1)
-        s_bell(2)
+        s_square_b(2)
+        s_square_b(3)
+        s_rest(2)
         copy_a(nc.scalar.copy, 2)
-        s_bell(3)
+        s_rest(3)
         copy_a(nc.scalar.copy, 3)
-        product(bank_a[0], 0, w1_q, dx_q)
-        product(bank_a[1], 1, w1_q, dx_q)
+        g_square_a(0)
+        g_square_a(1)
+        ta_to_a(0)
         v_k1(0)
-        v_m1(0)
-        product(bank_a[2], 2, w1_q, dx_q)
+        tb_to_b(0)
+        ta_to_a(1)
         v_k1(1)
-        v_m1(1)
-        product(bank_a[3], 3, w1_q, dx_q)
+        tb_to_b(1)
+        v_m1(0)
+        tb_to_a(0)
         v_k2(0)
-        v_k1(2)
+        b_to_b(0)
+        g_dz(0)
+        v_m1(1)
+        tb_to_a(1)
         v_k2(1)
-        v_m1(2)
+        b_to_b(1)
+        g_dz(1)
+        g_square_a(2)
+        ta_to_a(2)
+        v_k1(2)
+        tb_to_b(2)
+        ta_to_a(3)
         v_k1(3)
-        v_m1(3)
+        tb_to_b(3)
+        v_m1(2)
+        tb_to_a(2)
         v_k2(2)
-        v_u(0)
+        b_to_b(2)
+        g_dz(2)
+        v_m1(3)
+        tb_to_a(3)
         v_k2(3)
+        b_to_b(3)
+        g_dz(3)
+        nc.scalar.activation(out=log_rest[0][:], in_=rest[0][:], func=ACT.Ln)
+        nc.scalar.activation(out=log_rest[1][:], in_=rest[1][:], func=ACT.Ln)
+        nc.scalar.activation(out=log_rest[2][:], in_=rest[2][:], func=ACT.Ln)
+        nc.scalar.activation(out=log_rest[3][:], in_=rest[3][:], func=ACT.Ln)
+        nc.scalar.activation(out=a_sq[3][:], in_=a_sb[3][:], func=ACT.Square)
+        v_u(0)
         v_u(1)
         v_u(2)
+        v_logit(0)
+        v_logit(1)
+        nc.scalar.activation(out=share[0][:], in_=logit[0][:], func=ACT.Sigmoid, scale=-1.0, bias=neg_log_fl[:, 0 : 0 + 1])
+        nc.scalar.activation(out=share[1][:], in_=logit[1][:], func=ACT.Sigmoid, scale=-1.0, bias=neg_log_fl[:, 1 : 1 + 1])
         v_u(3)
-
-        for g in range(G):
-            nc.scalar.activation(out=a_sq[g][:], in_=a_sb[g][:], func=ACT.Square)
-            nc.scalar.activation(out=log_rest[g][:], in_=rest[g][:], func=ACT.Ln)
-            nc.gpsimd.tensor_tensor(out=logit[g][:], in0=a_sq[g][:], in1=log_rest[g][:], op=ALU.subtract)
-        for g in range(G):
-            nc.scalar.activation(
-                out=share[g][:], in_=logit[g][:], func=ACT.Sigmoid, scale=-1.0, bias=neg_log_fl[:, g : g + 1]
-            )
+        v_logit(2)
+        v_logit(3)
+        nc.scalar.activation(out=share[2][:], in_=logit[2][:], func=ACT.Sigmoid, scale=-1.0, bias=neg_log_fl[:, 2 : 2 + 1])
+        nc.scalar.activation(out=share[3][:], in_=logit[3][:], func=ACT.Sigmoid, scale=-1.0, bias=neg_log_fl[:, 3 : 3 + 1])
 
         for pair in ((0, 1), (2, 3)):
             for g in pair:

@@ -17,7 +17,8 @@ P = 128
 PACK = 4
 ROWS = D // PACK
 RUN = 4
-X_SPLIT = 344
+HALF = N // 2
+X_SPLIT = 176
 SMALLEST_FLOOR = 2.0**-60
 
 
@@ -28,10 +29,18 @@ def tile_rows_tngaussshare_kernel(tc, x, w1, w2, fl, dx, og, base, out):
         ps = ctx.enter_context(tc.psum_pool(name="ps", bufs=1))
         ctx.enter_context(tc.manual_schedule())
 
-        def load_rows(name, src, width):
-            raw = sb.tile([P, PACK, width], F32, name=name + "_raw")
+        def load_rows(name, src):
+            raw = sb.tile([P, PACK, src.shape[2]], F32, name=name + "_raw")
             nc.sync.dma_start(out=raw[:], in_=src.rearrange("g (p j) n -> (g p) j n", j=PACK))
             return raw
+
+        def bf16_tile(name, width):
+            return sb.tile([P, width, PACK], BF16, name=name + "_bf", align_bytes=64)
+
+        def mx_tiles(name, width):
+            codes = sb.tile([P, width], U32, name=name + "_codes", align_bytes=64)
+            scales = sb.tile([P, width], U8, name=name + "_scales", align_bytes=64)
+            return codes, scales
 
         def interleave(copy, grouped, raw, lo, hi):
             copy(
@@ -39,15 +48,13 @@ def tile_rows_tngaussshare_kernel(tc, x, w1, w2, fl, dx, og, base, out):
                 in_=raw[:, :, lo:hi].rearrange("p j (c i) -> p c j i", i=RUN),
             )
 
-        def quantize(name, grouped, width):
-            codes = sb.tile([P, width], U32, name=name + "_codes", align_bytes=64)
-            scales = sb.tile([P, width], U8, name=name + "_scales", align_bytes=64)
+        def quantize(mx, first, grouped):
+            cols = slice(first, first + grouped.shape[1])
             nc.vector.quantize_mx(
-                out=codes[:].bitcast(FP8X4),
-                scales=scales[:],
+                out=mx[0][:, cols].bitcast(FP8X4),
+                scales=mx[1][:, cols],
                 in_=grouped[:].rearrange("p n j -> p (n j)"),
             )
-            return codes, scales
 
         def product(bank, g, weights, moving):
             rows = slice(ROWS * g, ROWS * (g + 1))
@@ -67,15 +74,15 @@ def tile_rows_tngaussshare_kernel(tc, x, w1, w2, fl, dx, og, base, out):
         small_rows = sb.tile([P, 2 * G * 32], F32, align_bytes=64)
         small_cols = sb.tile([P, 2 * G * 32], F32, align_bytes=64)
         nc.vector.memset(small_rows[:], 0.0)
-        w2_raw = load_rows("w2", w2, M)
+        w2_raw = load_rows("w2", w2)
         for k, vec in enumerate((fl, og)):
             nc.sync.dma_start(
                 out=small_rows[0:P:32, k * G * 32 : (k + 1) * G * 32].rearrange("q (g i) -> q g i", i=32),
                 in_=vec.rearrange("g (q i) o -> q g (i o)", i=32),
             )
-        x_raw = load_rows("x", x, N)
-        w1_raw = load_rows("w1", w1, M)
-        dx_raw = load_rows("dx", dx, N)
+        x_raw = [load_rows("x%d" % h, x[:, :, h * HALF : (h + 1) * HALF]) for h in range(2)]
+        w1_raw = load_rows("w1", w1)
+        dx_raw = [load_rows("dx%d" % h, dx[:, :, h * HALF : (h + 1) * HALF]) for h in range(2)]
         base_sb = sb.tile([P, G, N], F32)
         nc.sync.dma_start(out=base_sb[:], in_=base.rearrange("g m n -> m g n"))
 
@@ -83,32 +90,36 @@ def tile_rows_tngaussshare_kernel(tc, x, w1, w2, fl, dx, og, base, out):
             col = (G + g) * 32
             return small_cols[:, col : col + 1]
 
-        w2_bf = sb.tile([P, M, PACK], BF16, align_bytes=64)
-        w1_bf = sb.tile([P, M, PACK], BF16, align_bytes=64)
-        x_bf = sb.tile([P, N, PACK], BF16, align_bytes=64)
-        dx_bf = sb.tile([P, N, PACK], BF16, align_bytes=64)
+        w2_bf = bf16_tile("w2", M)
+        w1_bf = bf16_tile("w1", M)
+        x_bf = [bf16_tile("x%d" % h, HALF) for h in range(2)]
+        dx_bf = [bf16_tile("dx%d" % h, HALF) for h in range(2)]
+        w2_q = mx_tiles("w2", M)
+        w1_q = mx_tiles("w1", M)
+        x_q = mx_tiles("x", N)
+        dx_q = mx_tiles("dx", N)
 
         bank_b = [ps.tile([P, N], F32, name="bank_b%d" % g) for g in range(G)]
         bank_a = [ps.tile([P, N], F32, name="bank_a%d" % g) for g in range(G)]
 
-        floor = sb.tile([P, G], F32)
         log_fl = sb.tile([P, G], F32)
         neg_log_fl = sb.tile([P, G], F32)
         warm = sb.tile([P, 1], F32)
         nc.vector.transpose(small_cols[:], small_rows[:])
         interleave(nc.vector.tensor_copy, w2_bf, w2_raw, 0, M)
-        nc.vector.tensor_scalar_max(out=floor[:], in0=small_cols[:, 0 : G * 32 : 32], scalar1=SMALLEST_FLOOR)
-        w2_q = quantize("w2", w2_bf, M)
-        nc.scalar.activation(out=log_fl[:], in_=floor[:], func=ACT.Ln)
+        quantize(w2_q, 0, w2_bf)
+        nc.scalar.activation(out=log_fl[:], in_=small_cols[:, 0 : G * 32 : 32], func=ACT.Ln, bias=SMALLEST_FLOOR)
         nc.scalar.mul(out=neg_log_fl[:], in_=log_fl[:], mul=-1.0)
-        interleave(nc.vector.tensor_copy, x_bf, x_raw, 0, X_SPLIT)
-        interleave(nc.scalar.copy, x_bf, x_raw, X_SPLIT, N)
+        interleave(nc.vector.tensor_copy, x_bf[0], x_raw[0], 0, HALF)
+        quantize(x_q, 0, x_bf[0])
+        interleave(nc.vector.tensor_copy, x_bf[1], x_raw[1], 0, X_SPLIT)
+        interleave(nc.scalar.copy, x_bf[1], x_raw[1], X_SPLIT, HALF)
         nc.scalar.activation(out=warm[:], in_=log_fl[:, 0:1], func=ACT.Sigmoid)
-        interleave(nc.vector.tensor_copy, w1_bf, w1_raw, 0, M)
-        x_q = quantize("x", x_bf, N)
+        quantize(x_q, HALF, x_bf[1])
         for g in range(G):
             product(bank_b[g], g, w2_q, x_q)
-        w1_q = quantize("w1", w1_bf, M)
+        interleave(nc.vector.tensor_copy, w1_bf, w1_raw, 0, M)
+        quantize(w1_q, 0, w1_bf)
         for g in range(G):
             product(bank_a[g], g, w1_q, x_q)
 
@@ -175,9 +186,11 @@ def tile_rows_tngaussshare_kernel(tc, x, w1, w2, fl, dx, og, base, out):
         def b_to_b(g):
             product(bank_b[g], g, w2_q, x_q)
 
-        interleave(nc.vector.tensor_copy, dx_bf, dx_raw, 0, N)
+        interleave(nc.vector.tensor_copy, dx_bf[0], dx_raw[0], 0, HALF)
+        quantize(dx_q, 0, dx_bf[0])
+        interleave(nc.vector.tensor_copy, dx_bf[1], dx_raw[1], 0, HALF)
         copy_a(nc.vector.tensor_copy, 0)
-        dx_q = quantize("dx", dx_bf, N)
+        quantize(dx_q, HALF, dx_bf[1])
         s_square_b(0)
         s_square_b(1)
         s_rest(0)

@@ -17,9 +17,12 @@ P = 128
 PACK = 4
 ROWS = D // PACK
 RUN = 4
+BLOCK = 32
 HALF = N // 2
 X_SPLIT = 176
-SMALLEST_FLOOR = 2.0**-60
+LN_GUARD = 2.0**-60
+PAIRS = ((0, 1), (2, 3))
+LAST = G - 1
 
 
 def tile_rows_tngaussshare_kernel(tc, x, w1, w2, fl, dx, og, base, out):
@@ -71,24 +74,21 @@ def tile_rows_tngaussshare_kernel(tc, x, w1, w2, fl, dx, og, base, out):
         def per_group(name):
             return [sb.tile([P, N], F32, name="%s%d" % (name, g)) for g in range(G)]
 
-        small_rows = sb.tile([P, 2 * G * 32], F32, align_bytes=64)
-        small_cols = sb.tile([P, 2 * G * 32], F32, align_bytes=64)
-        nc.vector.memset(small_rows[:], 0.0)
+        vec_width = G * BLOCK
+        vec_rows = sb.tile([P, 2 * vec_width], F32, align_bytes=64)
+        vec_cols = sb.tile([P, 2 * vec_width], F32, align_bytes=64)
+        nc.vector.memset(vec_rows[:], 0.0)
         w2_raw = load_rows("w2", w2)
         for k, vec in enumerate((fl, og)):
             nc.sync.dma_start(
-                out=small_rows[0:P:32, k * G * 32 : (k + 1) * G * 32].rearrange("q (g i) -> q g i", i=32),
-                in_=vec.rearrange("g (q i) o -> q g (i o)", i=32),
+                out=vec_rows[0:P:BLOCK, k * vec_width : (k + 1) * vec_width].rearrange("q (g i) -> q g i", i=BLOCK),
+                in_=vec.rearrange("g (q i) o -> q g (i o)", i=BLOCK),
             )
         x_raw = [load_rows("x%d" % h, x[:, :, h * HALF : (h + 1) * HALF]) for h in range(2)]
         w1_raw = load_rows("w1", w1)
         dx_raw = [load_rows("dx%d" % h, dx[:, :, h * HALF : (h + 1) * HALF]) for h in range(2)]
         base_sb = sb.tile([P, G, N], F32)
         nc.sync.dma_start(out=base_sb[:], in_=base.rearrange("g m n -> m g n"))
-
-        def gain(g):
-            col = (G + g) * 32
-            return small_cols[:, col : col + 1]
 
         w2_bf = bf16_tile("w2", M)
         w1_bf = bf16_tile("w1", M)
@@ -99,173 +99,154 @@ def tile_rows_tngaussshare_kernel(tc, x, w1, w2, fl, dx, og, base, out):
         x_q = mx_tiles("x", N)
         dx_q = mx_tiles("dx", N)
 
-        bank_b = [ps.tile([P, N], F32, name="bank_b%d" % g) for g in range(G)]
-        bank_a = [ps.tile([P, N], F32, name="bank_a%d" % g) for g in range(G)]
+        bank2 = [ps.tile([P, N], F32, name="bank2_%d" % g) for g in range(G)]
+        bank1 = [ps.tile([P, N], F32, name="bank1_%d" % g) for g in range(G)]
 
         log_fl = sb.tile([P, G], F32)
         neg_log_fl = sb.tile([P, G], F32)
-        warm = sb.tile([P, 1], F32)
-        nc.vector.transpose(small_cols[:], small_rows[:])
+        z2_sq = per_group("z2_sq")
+        floor_part = per_group("floor_part")
+        z1_sb = per_group("z1_sb")
+        z1_sq = per_group("z1_sq")
+        log_part = per_group("log_part")
+        share = per_group("share")
+        weighted_z2 = per_group("weighted_z2")
+        term1 = per_group("term1")
+        term2 = per_group("term2")
+        half_dl = per_group("half_dl")
+        dl_z2 = per_group("dl_z2")
+        damped = per_group("damped")
+        inner = per_group("inner")
+        change = per_group("change")
+        logit = [sb.tile([P, N], F32, name="logit%d" % g) for g in range(LAST)] + [dl_z2[1]]
+        result = [dl_z2[LAST]] + [sb.tile([P, N], F32, name="result%d" % g) for g in range(1, G)]
+
+        def square(dst, src):
+            nc.scalar.activation(out=dst[:], in_=src[:], func=ACT.Square)
+
+        def make_logit(engine, g):
+            engine.tensor_tensor(out=logit[g][:], in0=z1_sq[g][:], in1=log_part[g][:], op=ALU.subtract)
+
+        def make_share(g):
+            nc.scalar.activation(
+                out=share[g][:], in_=logit[g][:], func=ACT.Sigmoid, scale=-1.0, bias=neg_log_fl[:, g : g + 1]
+            )
+
+        def make_dl_z2(g):
+            nc.vector.scalar_tensor_tensor(
+                out=dl_z2[g][:], in0=half_dl[g][:], scalar=2.0, in1=bank2[g][:], op0=ALU.mult, op1=ALU.mult
+            )
+
+        def make_damped(g):
+            nc.vector.scalar_tensor_tensor(
+                out=damped[g][:], in0=share[g][:], scalar=-1.0, in1=dl_z2[g][:], op0=ALU.add, op1=ALU.mult
+            )
+
+        def make_inner(g):
+            nc.vector.tensor_tensor(out=inner[g][:], in0=damped[g][:], in1=bank1[g][:], op=ALU.add)
+
+        def make_change(g, cols):
+            gain_col = vec_width + BLOCK * g
+            nc.vector.scalar_tensor_tensor(
+                out=change[g][:, cols],
+                in0=inner[g][:, cols],
+                scalar=vec_cols[:, gain_col : gain_col + 1],
+                in1=share[g][:, cols],
+                op0=ALU.mult,
+                op1=ALU.mult,
+            )
+
+        def finish(engine, g, cols):
+            engine.tensor_tensor(out=result[g][:, cols], in0=change[g][:, cols], in1=base_sb[:, g, cols], op=ALU.add)
+            nc.sync.dma_start(out=out[g, :, cols], in_=result[g][:, cols])
+
+        nc.vector.transpose(vec_cols[:], vec_rows[:])
         interleave(nc.vector.tensor_copy, w2_bf, w2_raw, 0, M)
         quantize(w2_q, 0, w2_bf)
-        nc.scalar.activation(out=log_fl[:], in_=small_cols[:, 0 : G * 32 : 32], func=ACT.Ln, bias=SMALLEST_FLOOR)
+        nc.scalar.activation(out=log_fl[:], in_=vec_cols[:, 0:vec_width:BLOCK], func=ACT.Ln, bias=LN_GUARD)
         nc.scalar.mul(out=neg_log_fl[:], in_=log_fl[:], mul=-1.0)
         interleave(nc.vector.tensor_copy, x_bf[0], x_raw[0], 0, HALF)
         quantize(x_q, 0, x_bf[0])
         interleave(nc.vector.tensor_copy, x_bf[1], x_raw[1], 0, X_SPLIT)
         interleave(nc.scalar.copy, x_bf[1], x_raw[1], X_SPLIT, HALF)
+        warm = sb.tile([P, 1], F32)
         nc.scalar.activation(out=warm[:], in_=log_fl[:, 0:1], func=ACT.Sigmoid)
         quantize(x_q, HALF, x_bf[1])
         for g in range(G):
-            product(bank_b[g], g, w2_q, x_q)
+            product(bank2[g], g, w2_q, x_q)
         interleave(nc.vector.tensor_copy, w1_bf, w1_raw, 0, M)
         quantize(w1_q, 0, w1_bf)
         for g in range(G):
-            product(bank_a[g], g, w1_q, x_q)
-
-        b_sq = per_group("b_sq")
-        rest = per_group("rest")
-        a_sb = per_group("a_sb")
-        a_sq = per_group("a_sq")
-        log_rest = per_group("log_rest")
-        logit = per_group("logit")
-        share = per_group("share")
-        k1 = per_group("k1")
-        k2 = per_group("k2")
-        m1 = per_group("m1")
-        dz = per_group("dz")
-        u = per_group("u")
-        v = per_group("v")
-        w = per_group("w")
-        y = per_group("y")
-        res = per_group("res")
-
-        def s_square_b(g):
-            nc.scalar.activation(out=b_sq[g][:], in_=bank_b[g][:], func=ACT.Square)
-
-        def s_rest(g):
-            nc.scalar.activation(out=rest[g][:], in_=b_sq[g][:], func=ACT.Sigmoid, bias=log_fl[:, g : g + 1])
-
-        def copy_a(copy, g):
-            copy(out=a_sb[g][:], in_=bank_a[g][:])
-
-        def g_square_a(g):
-            nc.gpsimd.tensor_tensor(out=a_sq[g][:], in0=a_sb[g][:], in1=a_sb[g][:], op=ALU.mult)
-
-        def g_dz(g):
-            nc.gpsimd.tensor_tensor(out=dz[g][:], in0=k2[g][:], in1=m1[g][:], op=ALU.add)
-
-        def v_k1(g):
-            nc.vector.scalar_tensor_tensor(
-                out=k1[g][:], in0=rest[g][:], scalar=-1.0, in1=bank_b[g][:], op0=ALU.add, op1=ALU.mult
-            )
-
-        def v_m1(g):
-            nc.vector.tensor_tensor(out=m1[g][:], in0=a_sb[g][:], in1=bank_a[g][:], op=ALU.mult)
-
-        def v_k2(g):
-            nc.vector.tensor_tensor(out=k2[g][:], in0=k1[g][:], in1=bank_b[g][:], op=ALU.mult)
-
-        def v_u(g):
-            nc.vector.scalar_tensor_tensor(
-                out=u[g][:], in0=dz[g][:], scalar=2.0, in1=bank_b[g][:], op0=ALU.mult, op1=ALU.mult
-            )
-
-        def v_logit(g):
-            nc.vector.tensor_tensor(out=logit[g][:], in0=a_sq[g][:], in1=log_rest[g][:], op=ALU.subtract)
-
-        def ta_to_a(g):
-            product(bank_a[g], g, w1_q, dx_q)
-
-        def tb_to_a(g):
-            product(bank_a[g], g, w2_q, dx_q)
-
-        def tb_to_b(g):
-            product(bank_b[g], g, w2_q, dx_q)
-
-        def b_to_b(g):
-            product(bank_b[g], g, w2_q, x_q)
-
+            product(bank1[g], g, w1_q, x_q)
         interleave(nc.vector.tensor_copy, dx_bf[0], dx_raw[0], 0, HALF)
         quantize(dx_q, 0, dx_bf[0])
         interleave(nc.vector.tensor_copy, dx_bf[1], dx_raw[1], 0, HALF)
-        copy_a(nc.vector.tensor_copy, 0)
+        nc.vector.tensor_copy(out=z1_sb[0][:], in_=bank1[0][:])
         quantize(dx_q, HALF, dx_bf[1])
-        s_square_b(0)
-        s_square_b(1)
-        s_rest(0)
-        s_rest(1)
-        copy_a(nc.scalar.copy, 1)
-        s_square_b(2)
-        s_square_b(3)
-        s_rest(2)
-        copy_a(nc.scalar.copy, 2)
-        s_rest(3)
-        copy_a(nc.scalar.copy, 3)
-        g_square_a(0)
-        g_square_a(1)
-        ta_to_a(0)
-        v_k1(0)
-        tb_to_b(0)
-        ta_to_a(1)
-        v_k1(1)
-        tb_to_b(1)
-        v_m1(0)
-        tb_to_a(0)
-        v_k2(0)
-        b_to_b(0)
-        g_dz(0)
-        v_m1(1)
-        tb_to_a(1)
-        v_k2(1)
-        b_to_b(1)
-        g_dz(1)
-        g_square_a(2)
-        ta_to_a(2)
-        v_k1(2)
-        tb_to_b(2)
-        ta_to_a(3)
-        v_k1(3)
-        tb_to_b(3)
-        v_m1(2)
-        tb_to_a(2)
-        v_k2(2)
-        b_to_b(2)
-        g_dz(2)
-        v_m1(3)
-        tb_to_a(3)
-        v_k2(3)
-        b_to_b(3)
-        g_dz(3)
-        nc.scalar.activation(out=log_rest[0][:], in_=rest[0][:], func=ACT.Ln)
-        nc.scalar.activation(out=log_rest[1][:], in_=rest[1][:], func=ACT.Ln)
-        nc.scalar.activation(out=log_rest[2][:], in_=rest[2][:], func=ACT.Ln)
-        nc.scalar.activation(out=log_rest[3][:], in_=rest[3][:], func=ACT.Ln)
-        nc.scalar.activation(out=a_sq[3][:], in_=a_sb[3][:], func=ACT.Square)
-        v_u(0)
-        v_u(1)
-        v_u(2)
-        v_logit(0)
-        v_logit(1)
-        nc.scalar.activation(out=share[0][:], in_=logit[0][:], func=ACT.Sigmoid, scale=-1.0, bias=neg_log_fl[:, 0 : 0 + 1])
-        nc.scalar.activation(out=share[1][:], in_=logit[1][:], func=ACT.Sigmoid, scale=-1.0, bias=neg_log_fl[:, 1 : 1 + 1])
-        v_u(3)
-        v_logit(2)
-        v_logit(3)
-        nc.scalar.activation(out=share[2][:], in_=logit[2][:], func=ACT.Sigmoid, scale=-1.0, bias=neg_log_fl[:, 2 : 2 + 1])
-        nc.scalar.activation(out=share[3][:], in_=logit[3][:], func=ACT.Sigmoid, scale=-1.0, bias=neg_log_fl[:, 3 : 3 + 1])
 
-        for pair in ((0, 1), (2, 3)):
+        for pair in PAIRS:
             for g in pair:
-                nc.vector.scalar_tensor_tensor(
-                    out=v[g][:], in0=share[g][:], scalar=-1.0, in1=u[g][:], op0=ALU.add, op1=ALU.mult
+                square(z2_sq[g], bank2[g])
+            for g in pair:
+                nc.scalar.activation(
+                    out=floor_part[g][:], in_=z2_sq[g][:], func=ACT.Sigmoid, bias=log_fl[:, g : g + 1]
                 )
+                if g > 0:
+                    nc.scalar.copy(out=z1_sb[g][:], in_=bank1[g][:])
+
+        for pair in PAIRS:
             for g in pair:
-                nc.vector.tensor_tensor(out=w[g][:], in0=v[g][:], in1=bank_a[g][:], op=ALU.add)
+                if g < LAST:
+                    nc.gpsimd.tensor_tensor(out=z1_sq[g][:], in0=z1_sb[g][:], in1=z1_sb[g][:], op=ALU.mult)
             for g in pair:
+                product(bank1[g], g, w1_q, dx_q)
                 nc.vector.scalar_tensor_tensor(
-                    out=y[g][:], in0=w[g][:], scalar=gain(g), in1=share[g][:], op0=ALU.mult, op1=ALU.mult
+                    out=weighted_z2[g][:],
+                    in0=floor_part[g][:],
+                    scalar=-1.0,
+                    in1=bank2[g][:],
+                    op0=ALU.add,
+                    op1=ALU.mult,
                 )
+                product(bank2[g], g, w2_q, dx_q)
             for g in pair:
-                nc.vector.tensor_tensor(out=res[g][:], in0=y[g][:], in1=base_sb[:, g, :], op=ALU.add)
-                nc.sync.dma_start(out=out[g], in_=res[g][:])
+                nc.vector.tensor_tensor(out=term1[g][:], in0=z1_sb[g][:], in1=bank1[g][:], op=ALU.mult)
+                product(bank1[g], g, w2_q, dx_q)
+                nc.vector.tensor_tensor(out=term2[g][:], in0=weighted_z2[g][:], in1=bank2[g][:], op=ALU.mult)
+                product(bank2[g], g, w2_q, x_q)
+                nc.gpsimd.tensor_tensor(out=half_dl[g][:], in0=term2[g][:], in1=term1[g][:], op=ALU.add)
+
+        for g in range(G):
+            nc.scalar.activation(out=log_part[g][:], in_=floor_part[g][:], func=ACT.Ln)
+        for g in range(LAST):
+            make_dl_z2(g)
+        for g in range(LAST):
+            make_logit(nc.vector, g)
+        first, second = PAIRS
+        for g in first:
+            make_share(g)
+        square(z1_sq[LAST], z1_sb[LAST])
+        make_share(second[0])
+        for g in first:
+            make_damped(g)
+        make_logit(nc.gpsimd, LAST)
+        make_share(LAST)
+        make_dl_z2(LAST)
+        for g in first:
+            make_inner(g)
+        whole = slice(0, N)
+        for g in first:
+            make_change(g, whole)
+        for g in second:
+            make_damped(g)
+        finish(nc.gpsimd, 0, whole)
+        for g in second:
+            make_inner(g)
+        make_change(second[0], whole)
+        finish(nc.vector, first[1], whole)
+        finish(nc.vector, second[0], whole)
+        halves = (slice(0, HALF), slice(HALF, N))
+        for cols in halves:
+            make_change(LAST, cols)
+        for cols in halves:
+            finish(nc.vector, LAST, cols)

from contextlib import ExitStack

import concourse.mybir as mybir

G, D, M, N = 4, 128, 128, 512
FLOPS = 4 * 2 * G * D * M * N

F32 = mybir.dt.float32
BF16 = mybir.dt.bfloat16
U32 = mybir.dt.uint32
U8 = mybir.dt.uint8
FP8X4 = mybir.dt.float8_e4m3fn_x4
ALU = mybir.AluOpType
ACT = mybir.ActivationFunctionType

P = 128
PACK = 4
ROWS = D // PACK
RUN = 4
BLOCK = 32
HALF = N // 2
X_SPLIT = 176
LN_GUARD = 2.0**-60
PAIRS = ((0, 1), (2, 3))
LAST = G - 1


def tile_rows_tngaussshare_kernel(tc, x, w1, w2, fl, dx, og, base, out):
    nc = tc.nc
    with ExitStack() as ctx:
        sb = ctx.enter_context(tc.tile_pool(name="sb", bufs=1))
        ps = ctx.enter_context(tc.psum_pool(name="ps", bufs=1))
        ctx.enter_context(tc.manual_schedule())

        def load_rows(name, src):
            raw = sb.tile([P, PACK, src.shape[2]], F32, name=name + "_raw")
            nc.sync.dma_start(out=raw[:], in_=src.rearrange("g (p j) n -> (g p) j n", j=PACK))
            return raw

        def bf16_tile(name, width):
            return sb.tile([P, width, PACK], BF16, name=name + "_bf", align_bytes=64)

        def mx_tiles(name, width):
            codes = sb.tile([P, width], U32, name=name + "_codes", align_bytes=64)
            scales = sb.tile([P, width], U8, name=name + "_scales", align_bytes=64)
            return codes, scales

        def interleave(copy, grouped, raw, lo, hi):
            copy(
                out=grouped[:, lo:hi, :].rearrange("p (c i) j -> p c j i", i=RUN),
                in_=raw[:, :, lo:hi].rearrange("p j (c i) -> p c j i", i=RUN),
            )

        def quantize(mx, first, grouped):
            cols = slice(first, first + grouped.shape[1])
            nc.vector.quantize_mx(
                out=mx[0][:, cols].bitcast(FP8X4),
                scales=mx[1][:, cols],
                in_=grouped[:].rearrange("p n j -> p (n j)"),
            )

        def product(bank, g, weights, moving):
            rows = slice(ROWS * g, ROWS * (g + 1))
            nc.tensor.matmul_mx(
                out=bank[:],
                lhsT=weights[0][rows, :].bitcast(FP8X4),
                lhsT_scale=weights[1][rows, :],
                rhs=moving[0][rows, :].bitcast(FP8X4),
                rhs_scale=moving[1][rows, :],
                start=True,
                stop=True,
            )

        def per_group(name):
            return [sb.tile([P, N], F32, name="%s%d" % (name, g)) for g in range(G)]

        vec_width = G * BLOCK
        vec_rows = sb.tile([P, 2 * vec_width], F32, align_bytes=64)
        vec_cols = sb.tile([P, 2 * vec_width], F32, align_bytes=64)
        nc.vector.memset(vec_rows[:], 0.0)
        w2_raw = load_rows("w2", w2)
        for k, vec in enumerate((fl, og)):
            nc.sync.dma_start(
                out=vec_rows[0:P:BLOCK, k * vec_width : (k + 1) * vec_width].rearrange("q (g i) -> q g i", i=BLOCK),
                in_=vec.rearrange("g (q i) o -> q g (i o)", i=BLOCK),
            )
        x_raw = [load_rows("x%d" % h, x[:, :, h * HALF : (h + 1) * HALF]) for h in range(2)]
        w1_raw = load_rows("w1", w1)
        dx_raw = [load_rows("dx%d" % h, dx[:, :, h * HALF : (h + 1) * HALF]) for h in range(2)]
        base_sb = sb.tile([P, G, N], F32)
        nc.sync.dma_start(out=base_sb[:], in_=base.rearrange("g m n -> m g n"))

        w2_bf = bf16_tile("w2", M)
        w1_bf = bf16_tile("w1", M)
        x_bf = [bf16_tile("x%d" % h, HALF) for h in range(2)]
        dx_bf = [bf16_tile("dx%d" % h, HALF) for h in range(2)]
        w2_q = mx_tiles("w2", M)
        w1_q = mx_tiles("w1", M)
        x_q = mx_tiles("x", N)
        dx_q = mx_tiles("dx", N)

        bank2 = [ps.tile([P, N], F32, name="bank2_%d" % g) for g in range(G)]
        bank1 = [ps.tile([P, N], F32, name="bank1_%d" % g) for g in range(G)]

        log_fl = sb.tile([P, G], F32)
        neg_log_fl = sb.tile([P, G], F32)
        z2_sq = per_group("z2_sq")
        floor_part = per_group("floor_part")
        z1_sb = per_group("z1_sb")
        z1_sq = per_group("z1_sq")
        log_part = per_group("log_part")
        share = per_group("share")
        weighted_z2 = per_group("weighted_z2")
        term1 = per_group("term1")
        term2 = per_group("term2")
        half_dl = per_group("half_dl")
        dl_z2 = per_group("dl_z2")
        damped = per_group("damped")
        inner = per_group("inner")
        change = per_group("change")
        logit = [sb.tile([P, N], F32, name="logit%d" % g) for g in range(LAST)] + [dl_z2[1]]
        result = [dl_z2[LAST]] + [sb.tile([P, N], F32, name="result%d" % g) for g in range(1, G)]

        def square(dst, src):
            nc.scalar.activation(out=dst[:], in_=src[:], func=ACT.Square)

        def make_logit(engine, g):
            engine.tensor_tensor(out=logit[g][:], in0=z1_sq[g][:], in1=log_part[g][:], op=ALU.subtract)

        def make_share(g):
            nc.scalar.activation(
                out=share[g][:], in_=logit[g][:], func=ACT.Sigmoid, scale=-1.0, bias=neg_log_fl[:, g : g + 1]
            )

        def make_dl_z2(g):
            nc.vector.scalar_tensor_tensor(
                out=dl_z2[g][:], in0=half_dl[g][:], scalar=2.0, in1=bank2[g][:], op0=ALU.mult, op1=ALU.mult
            )

        def make_damped(g):
            nc.vector.scalar_tensor_tensor(
                out=damped[g][:], in0=share[g][:], scalar=-1.0, in1=dl_z2[g][:], op0=ALU.add, op1=ALU.mult
            )

        def make_inner(g):
            nc.vector.tensor_tensor(out=inner[g][:], in0=damped[g][:], in1=bank1[g][:], op=ALU.add)

        def make_change(g, cols):
            gain_col = vec_width + BLOCK * g
            nc.vector.scalar_tensor_tensor(
                out=change[g][:, cols],
                in0=inner[g][:, cols],
                scalar=vec_cols[:, gain_col : gain_col + 1],
                in1=share[g][:, cols],
                op0=ALU.mult,
                op1=ALU.mult,
            )

        def finish(engine, g, cols):
            engine.tensor_tensor(out=result[g][:, cols], in0=change[g][:, cols], in1=base_sb[:, g, cols], op=ALU.add)
            nc.sync.dma_start(out=out[g, :, cols], in_=result[g][:, cols])

        nc.vector.transpose(vec_cols[:], vec_rows[:])
        interleave(nc.vector.tensor_copy, w2_bf, w2_raw, 0, M)
        quantize(w2_q, 0, w2_bf)
        nc.scalar.activation(out=log_fl[:], in_=vec_cols[:, 0:vec_width:BLOCK], func=ACT.Ln, bias=LN_GUARD)
        nc.scalar.mul(out=neg_log_fl[:], in_=log_fl[:], mul=-1.0)
        interleave(nc.vector.tensor_copy, x_bf[0], x_raw[0], 0, HALF)
        quantize(x_q, 0, x_bf[0])
        interleave(nc.vector.tensor_copy, x_bf[1], x_raw[1], 0, X_SPLIT)
        interleave(nc.scalar.copy, x_bf[1], x_raw[1], X_SPLIT, HALF)
        warm = sb.tile([P, 1], F32)
        nc.scalar.activation(out=warm[:], in_=log_fl[:, 0:1], func=ACT.Sigmoid)
        quantize(x_q, HALF, x_bf[1])
        for g in range(G):
            product(bank2[g], g, w2_q, x_q)
        interleave(nc.vector.tensor_copy, w1_bf, w1_raw, 0, M)
        quantize(w1_q, 0, w1_bf)
        for g in range(G):
            product(bank1[g], g, w1_q, x_q)
        interleave(nc.vector.tensor_copy, dx_bf[0], dx_raw[0], 0, HALF)
        quantize(dx_q, 0, dx_bf[0])
        interleave(nc.vector.tensor_copy, dx_bf[1], dx_raw[1], 0, HALF)
        nc.vector.tensor_copy(out=z1_sb[0][:], in_=bank1[0][:])
        quantize(dx_q, HALF, dx_bf[1])

        for pair in PAIRS:
            for g in pair:
                square(z2_sq[g], bank2[g])
            for g in pair:
                nc.scalar.activation(
                    out=floor_part[g][:], in_=z2_sq[g][:], func=ACT.Sigmoid, bias=log_fl[:, g : g + 1]
                )
                if g > 0:
                    nc.scalar.copy(out=z1_sb[g][:], in_=bank1[g][:])

        for pair in PAIRS:
            for g in pair:
                if g < LAST:
                    nc.gpsimd.tensor_tensor(out=z1_sq[g][:], in0=z1_sb[g][:], in1=z1_sb[g][:], op=ALU.mult)
            for g in pair:
                product(bank1[g], g, w1_q, dx_q)
                nc.vector.scalar_tensor_tensor(
                    out=weighted_z2[g][:],
                    in0=floor_part[g][:],
                    scalar=-1.0,
                    in1=bank2[g][:],
                    op0=ALU.add,
                    op1=ALU.mult,
                )
                product(bank2[g], g, w2_q, dx_q)
            for g in pair:
                nc.vector.tensor_tensor(out=term1[g][:], in0=z1_sb[g][:], in1=bank1[g][:], op=ALU.mult)
                product(bank1[g], g, w2_q, dx_q)
                nc.vector.tensor_tensor(out=term2[g][:], in0=weighted_z2[g][:], in1=bank2[g][:], op=ALU.mult)
                product(bank2[g], g, w2_q, x_q)
                nc.gpsimd.tensor_tensor(out=half_dl[g][:], in0=term2[g][:], in1=term1[g][:], op=ALU.add)

        for g in range(G):
            nc.scalar.activation(out=log_part[g][:], in_=floor_part[g][:], func=ACT.Ln)
        for g in range(LAST):
            make_dl_z2(g)
        for g in range(LAST):
            make_logit(nc.vector, g)
        first, second = PAIRS
        for g in first:
            make_share(g)
        square(z1_sq[LAST], z1_sb[LAST])
        make_share(second[0])
        for g in first:
            make_damped(g)
        make_logit(nc.gpsimd, LAST)
        make_share(LAST)
        make_dl_z2(LAST)
        for g in first:
            make_inner(g)
        whole = slice(0, N)
        for g in first:
            make_change(g, whole)
        for g in second:
            make_damped(g)
        finish(nc.gpsimd, 0, whole)
        for g in second:
            make_inner(g)
        make_change(second[0], whole)
        finish(nc.vector, first[1], whole)
        finish(nc.vector, second[0], whole)
        halves = (slice(0, HALF), slice(HALF, N))
        for cols in halves:
            make_change(LAST, cols)
        for cols in halves:
            finish(nc.vector, LAST, cols)
